import numpy as np
import ml_dtypes


def mxq(x, axis, fmt="e4m3"):
    dtype, down = {"e4m3": (ml_dtypes.float8_e4m3fn, 7), "e5m2": (ml_dtypes.float8_e5m2, 14)}[fmt]
    v = np.moveaxis(np.asarray(x, np.float32).astype(ml_dtypes.bfloat16).astype(np.float64), axis, -1)
    blocks = v.reshape(v.shape[:-1] + (-1, 32))
    amax = np.abs(blocks).max(-1, keepdims=True)
    byte = np.maximum(np.where(amax > 0, np.frexp(amax)[1] - 1 + 127, 0) - down, 1)
    scale = np.exp2(byte - 127.0)
    codes = (blocks / scale).astype(np.float32).astype(dtype).astype(np.float64)
    return np.moveaxis((codes * scale).reshape(v.shape), -1, axis)


WIDE = False


def mx_kscale(k):
    if not WIDE:
        return np.ones(k)
    levels = np.array([10, -10, 5, -5, 0])
    if k % 512:
        return np.exp2(np.random.permutation(np.resize(levels, k // 32))).repeat(32)
    a = np.empty((k // 512, 16))
    for p in range(k // 512):
        a[p, :8] = np.random.permutation(np.resize(levels, 8))
        for g in range(8):
            far = levels[np.abs(levels - a[p, g]) >= 10]
            a[p, g + 8] = far[np.random.randint(len(far))]
    return np.exp2(a.ravel()).repeat(32)


def f64(x):
    return np.asarray(x).astype(np.float64)


def striped(idx):
    return np.tile(np.asarray(idx).reshape(-1, 16).T, (8, 1)).astype(np.uint16)


def unstriped(offs):
    return offs[:16].T.reshape(-1).astype(np.int64)


E2M1 = np.array([0.0, 0.5, 1.0, 1.5, 2.0, 3.0, 4.0, 6.0, -0.0, -0.5, -1.0, -1.5, -2.0, -3.0, -4.0, -6.0])


def pack_weight(w, fmt):
    k, n = w.shape
    w = f64(np.asarray(w, np.float32).astype(ml_dtypes.bfloat16)).reshape(k // 32, 32, n)
    amax = np.abs(w).max(1)
    if fmt == "e4m3":
        byte = np.frexp(amax)[1] - 1 + 127 - 7
    else:
        mant, ex = np.frexp(amax / 6.0)
        byte = np.where(mant > 0.5, ex, ex - 1) + 127
    byte = np.clip(np.where(amax > 0, byte, 1), 1, 254)
    scaled = (w * np.exp2(127.0 - byte)[:, None, :]).reshape(k, n).astype(np.float32)
    by_word = np.ascontiguousarray(scaled.reshape(k // 512, 128, 4, n).transpose(0, 1, 3, 2))
    if fmt == "e4m3":
        words = by_word.astype(ml_dtypes.float8_e4m3fn).view(np.uint8)
    else:
        c = by_word.astype(ml_dtypes.float4_e2m1fn).view(np.uint8) & 0xF
        words = (c[..., 0::2] | (c[..., 1::2] << 4)).reshape(k // 512, 128, 2 * n)
    return np.ascontiguousarray(words), np.ascontiguousarray(byte.astype(np.uint8).reshape(k // 512, 16, n))


def unpack_weight(words, scales, fmt):
    g, _, n = scales.shape
    words = np.ascontiguousarray(words).reshape(g, 128, n, -1)
    if fmt == "e4m3":
        vals = words.view(ml_dtypes.float8_e4m3fn).astype(np.float64)
    else:
        nib = np.empty((g, 128, n, 4), np.uint8)
        nib[..., 0::2] = words & 0xF
        nib[..., 1::2] = words >> 4
        vals = E2M1[nib]
    vals = vals * np.repeat(np.exp2(scales.astype(np.float64) - 127.0), 8, axis=1)[..., None]
    return vals.transpose(0, 1, 3, 2).reshape(g * 512, n)


D, E, T, I, U, Q = 512, 512, 2048, 256, 1024, 512


def setup_inputs():
    n = np.random.standard_normal
    idx = np.random.permutation(T)[:I]
    idx2 = np.random.permutation(U)[:I]
    fd = mx_kscale(D)
    fe = mx_kscale(E)
    fq = mx_kscale(Q)
    keysp = pack_weight(n((D, T)) / fd[:, None], "e4m3")
    valsp = pack_weight(n((E, T)) / fe[:, None], "e4m3")
    return {
        "query": (n((D, Q)) * 0.5 / np.sqrt(D) * fd[:, None]).astype(np.float32),
        "keys_words": keysp[0],
        "keys_scales": keysp[1],
        "gout": (n((E, Q)) * 1 / np.sqrt(E) * fe[:, None]).astype(np.float32),
        "vals_words": valsp[0],
        "vals_scales": valsp[1],
        "lse": (np.random.uniform(6.2, 6.5, (Q, 1))).astype(np.float32),
        "delta": (np.random.uniform(-0.3, 0.3, (Q, 1))).astype(np.float32),
        "qs": (np.random.uniform(100.0, 400.0, (Q, 1)) * fq[:, None]).astype(np.float32),
        "qrows": (n((Q, D)) / fq[:, None]).astype(np.float32),
        "old": (n((D, U)) * 4.0).astype(np.float32),
        "fade": (np.random.uniform(0.5, 1.0, (1, U))).astype(np.float32),
        "offs": striped(idx),
        "offs2": striped(idx2),
    }


def reference(query, keys_words, keys_scales, gout, vals_words, vals_scales, lse, delta, qs, qrows, old, fade, offs, offs2):
    idx = unstriped(offs)
    idx2 = unstriped(offs2)
    keysu = unpack_weight(keys_words, keys_scales, "e4m3")
    valsu = unpack_weight(vals_words, vals_scales, "e4m3")
    queryq = mxq(f64(query), 0, "e4m3")
    keysidxg = keysu[:, idx]
    a = queryq.T @ keysidxg
    goutq = mxq(f64(gout), 0, "e4m3")
    valsidxg = valsu[:, idx]
    dp = goutq.T @ valsidxg
    ds = np.exp(a - f64(lse)) * (dp - f64(delta)) * f64(qs)
    qrowsq = mxq(f64(qrows), 0, "e4m3")
    dsq = mxq(ds, 0, "e4m3")
    dk = qrowsq.T @ dsq
    df = np.zeros((D, U))
    df[:, idx2] = dk
    y = f64(old) * f64(fade) + df
    return y

@@ -1,0 +1,196 @@
+from contextlib import ExitStack
+
+import concourse.mybir as mybir
+from concourse.masks import make_identity
+
+D, E, T, I, U, Q = 512, 512, 2048, 256, 1024, 512
+FLOPS = 2 * Q * I * D + 2 * Q * I * E + 2 * D * I * Q
+
+F32 = mybir.dt.float32
+BF16 = mybir.dt.bfloat16
+I32 = mybir.dt.int32
+U32 = mybir.dt.uint32
+U16 = mybir.dt.uint16
+U8 = mybir.dt.uint8
+FP8X4 = mybir.dt.float8_e4m3fn_x4
+ALU = mybir.AluOpType
+ACT = mybir.ActivationFunctionType
+
+P = 128
+PACK = 4
+BANK = 512
+UB = U // P
+VALS_PLANE = 4
+HALF = D // 2
+
+
+def tile_attend_gkeystore_kernel(tc, query, keys_words, keys_scales, gout, vals_words, vals_scales,
+                                  lse, delta, qs, qrows, old, fade, offs, offs2, out):
+    nc = tc.nc
+    with ExitStack() as ctx:
+        lists = ctx.enter_context(tc.tile_pool(name="lists", bufs=1))
+        sb = ctx.enter_context(tc.tile_pool(name="sb", bufs=1))
+        ps = ctx.enter_context(tc.psum_pool(name="ps", bufs=1))
+
+        def load_rows(name, src, width):
+            raw = sb.tile([P, PACK, width], F32, name=name)
+            nc.sync.dma_start(out=raw[:], in_=src.rearrange("(p j) w -> p j w", j=PACK))
+            return raw
+
+        def load_words(name, src):
+            words = sb.tile([P, T], U32, name=name)
+            nc.sync.dma_start(out=words[:].bitcast(I32), in_=src[0].rearrange("p n t -> p (n t)").bitcast(I32))
+            return words
+
+        def load_scales(name, src, first):
+            plane = sb.tile([P, T], U8, name=name)
+            nc.vector.memset(plane[:].bitcast(I32), 0)
+            for f in range(4):
+                nc.sync.dma_start(out=plane[first + f : P : 32, :].bitcast(I32), in_=src[0, f : 16 : 4, :].bitcast(I32))
+            return plane
+
+        def load_column(name, src):
+            col = sb.tile([P, PACK], F32, name=name)
+            nc.sync.dma_start(out=col[:], in_=src.rearrange("(p t) o -> p (t o)", t=PACK))
+            return col
+
+        def quantize(name, grouped, width):
+            codes = sb.tile([P, width], U32, name=name + "_codes", align_bytes=64)
+            scales = sb.tile([P, width], U8, name=name + "_scales", align_bytes=64)
+            nc.vector.quantize_mx(out=codes[:].bitcast(FP8X4), scales=scales[:], in_=grouped[:])
+            return codes, scales
+
+        def deal(name, raw):
+            grouped = sb.tile([P, PACK * Q], BF16, name=name + "_bf16", align_bytes=64)
+            nc.vector.tensor_copy(
+                out=grouped[:].rearrange("p (t s j) -> p s j t", t=PACK, j=PACK),
+                in_=raw[:].rearrange("p j (s t) -> p s j t", t=PACK),
+            )
+            return quantize(name, grouped, Q)
+
+        def gather(name, words, plane):
+            codes = sb.tile([P, I], U32, name=name + "_codes", align_bytes=64)
+            scales = sb.tile([P, I], U8, name=name + "_scales", align_bytes=64)
+            nc.vector.tensor_copy(out=scales[:], in_=plane[:].indirect(slots[:]))
+            nc.vector.tensor_copy(out=codes[:], in_=words[:].indirect(slots[:]))
+            return codes, scales
+
+        def scores(name, lhs, rhs, first):
+            banks = [ps.tile([P, 2, I], F32, name=name + str(h), tag="mx" + str(h)) for h in range(2)]
+            outs = []
+            for t in range(PACK):
+                cols = slice(t * P, (t + 1) * P)
+                o = banks[t // 2][:, t % 2, :]
+                nc.tensor.matmul_mx(out=o, lhsT=lhs[t][0].bitcast(FP8X4), lhsT_scale=lhs[t][1],
+                                    rhs=rhs[0][:].bitcast(FP8X4), rhs_scale=rhs[1][first:P, :], start=True, stop=True)
+                outs.append(o)
+            return outs
+
+        def blocks(pair, n):
+            return [(pair[0][:, b * P : (b + 1) * P], pair[1][:, b * P : (b + 1) * P]) for b in range(n)]
+
+        gout_raw = load_rows("gout_raw", gout, Q)
+        vals_plane = load_scales("vals_plane", vals_scales, VALS_PLANE)
+        slots = lists.tile([P, I // 16], U16, name="slots")
+        nc.sync.dma_start(slots[:], offs)
+        vals_pool = load_words("vals_pool", vals_words)
+        lse_c = load_column("lse_c", lse)
+        delta_c = load_column("delta_c", delta)
+        qs_c = load_column("qs_c", qs)
+        query_raw = load_rows("query_raw", query, Q)
+        keys_plane = load_scales("keys_plane", keys_scales, 0)
+        keys_pool = load_words("keys_pool", keys_words)
+        qrows_raw = [load_rows("qrows_raw" + str(h), qrows[:, h * HALF : (h + 1) * HALF], HALF) for h in range(2)]
+        places = lists.tile([P, I // 16], U16, name="places")
+        nc.sync.dma_start(places[:], offs2)
+        fade_rows = sb.tile([P, P], F32, name="fade_rows")
+        nc.sync.dma_start(out=fade_rows[:], in_=fade.rearrange("o (b u) -> o b u", u=P).to_broadcast([P // UB, UB, P]))
+        old_t = []
+        for j in range(PACK):
+            o = sb.tile([P, U], F32, name="old" + str(j))
+            nc.sync.dma_start(out=o[:], in_=old[j * P : (j + 1) * P, :])
+            old_t.append(o)
+
+        windows = []
+        for j in range(2):
+            w = sb.tile([P, U], F32, name="window" + str(j))
+            nc.vector.memset(w[:], 0.0)
+            windows.append(w)
+        ident = sb.tile([P, P], F32, name="ident")
+        make_identity(nc, ident[:])
+        neg_lse = sb.tile([P, PACK], F32, name="neg_lse")
+        nc.scalar.activation(out=neg_lse[:], in_=lse_c[:], func=ACT.Copy, scale=-1.0)
+        fade_ps = ps.tile([P, PACK, P], F32, name="fade_ps", tag="turn0")
+        nc.tensor.transpose(fade_ps[:, 0, :], fade_rows[:], ident[:])
+        fade_c = sb.tile([P, UB], F32, name="fade_c")
+        nc.vector.tensor_copy(out=fade_c[:], in_=fade_ps[:, 0, 0:UB])
+
+        gout_q = deal("gout", gout_raw)
+        vals_g = gather("vals", vals_pool, vals_plane)
+        dp = scores("dp", blocks(gout_q, PACK), vals_g, VALS_PLANE)
+        grad = sb.tile([P, PACK, I], F32, name="grad")
+        for t in range(PACK):
+            nc.vector.tensor_scalar(out=grad[:, t, :], in0=dp[t], scalar1=delta_c[:, t : t + 1], scalar2=qs_c[:, t : t + 1],
+                                    op0=ALU.subtract, op1=ALU.mult)
+
+        query_q = deal("query", query_raw)
+        keys_g = gather("keys", keys_pool, keys_plane)
+        a = scores("a", blocks(query_q, PACK), keys_g, 0)
+        weight = sb.tile([P, PACK, I], F32, name="weight")
+        for t in range(PACK):
+            nc.scalar.activation(out=weight[:, t, :], in_=a[t], func=ACT.Exp, bias=neg_lse[:, t : t + 1], scale=1.0)
+
+        def weave(h, engine_copy):
+            grouped = sb.tile([P, PACK * HALF], BF16, name="qrows_bf16_" + str(h), align_bytes=64)
+            engine_copy(
+                out=grouped[:].rearrange("p (c i j) -> p c j i", i=4, j=PACK),
+                in_=qrows_raw[h][:].rearrange("p j (c i) -> p c j i", i=4),
+            )
+            return grouped
+
+        qrows_q = [quantize("qrows0", weave(0, nc.vector.tensor_copy), HALF)]
+
+        ds = sb.tile([P, PACK * I], BF16, name="ds", align_bytes=64)
+        nc.vector.tensor_tensor(
+            out=ds[:].rearrange("p (c i t) -> p c t i", i=4, t=PACK),
+            in0=weight[:].rearrange("p t (c i) -> p c t i", i=4),
+            in1=grad[:].rearrange("p t (c i) -> p c t i", i=4),
+            op=ALU.mult,
+        )
+        ds_q = quantize("ds", ds, I)
+        qrows_q.append(quantize("qrows1", weave(1, nc.scalar.copy), HALF))
+        dk = scores("dk", blocks(qrows_q[0], 2) + blocks(qrows_q[1], 2), ds_q, 0)
+
+        dk_sb = []
+        for j in range(PACK):
+            d = sb.tile([P, I], F32, name="dk_sb" + str(j))
+            nc.scalar.copy(out=d[:], in_=dk[j])
+            dk_sb.append(d)
+
+        def scatter(j):
+            nc.vector.tensor_copy(out=windows[j % 2][:].indirect(places[:]), in_=dk_sb[j][:])
+
+        def finish(j):
+            faded_t = sb.tile([P, UB, P], F32, name="faded_t" + str(j))
+            for h in range(2):
+                turn = ps.tile([P, PACK, P], F32, name="turn", tag="turn" + str(h))
+                for b in range(PACK):
+                    ub = h * PACK + b
+                    nc.tensor.transpose(turn[:, b, :], old_t[j][:, ub * P : (ub + 1) * P], ident[:])
+                for b in range(PACK):
+                    ub = h * PACK + b
+                    nc.scalar.activation(out=faded_t[:, ub, :], in_=turn[:, b, :], func=ACT.Copy, scale=fade_c[:, ub : ub + 1])
+            for h in range(2):
+                back = ps.tile([P, BANK], F32, name="back", tag="back" + str(2 * (j % 2) + h))
+                for b in range(PACK):
+                    nc.tensor.transpose(back[:, b * P : (b + 1) * P], faded_t[:, h * PACK + b, :], ident[:])
+                cols = slice(h * BANK, (h + 1) * BANK)
+                res = sb.tile([P, BANK], F32, name="res" + str(2 * j + h))
+                nc.vector.tensor_tensor(out=res[:], in0=back[:], in1=windows[j % 2][:, cols], op=ALU.add)
+                nc.sync.dma_start(out=out[j * P : (j + 1) * P, cols], in_=res[:])
+
+        scatter(0)
+        for j in range(PACK):
+            if j + 1 < PACK:
+                scatter(j + 1)
+            finish(j)

@@ -22,6 +22,8 @@ BANK = 512
 UB = U // P
 VALS_PLANE = 4
 HALF = D // 2
+SLOTS = I // 2
+DEAL_SPLIT = 80
 
 
 def tile_attend_gkeystore_kernel(tc, query, keys_words, keys_scales, gout, vals_words, vals_scales,
@@ -42,9 +44,9 @@ def tile_attend_gkeystore_kernel(tc, query, keys_words, keys_scales, gout, vals_
             nc.sync.dma_start(out=words[:].bitcast(I32), in_=src[0].rearrange("p n t -> p (n t)").bitcast(I32))
             return words
 
-        def load_scales(name, src, first):
+        def load_scales(name, src, first, clear):
             plane = sb.tile([P, T], U8, name=name)
-            nc.vector.memset(plane[:].bitcast(I32), 0)
+            clear.memset(plane[:].bitcast(I32), 0)
             for f in range(4):
                 nc.sync.dma_start(out=plane[first + f : P : 32, :].bitcast(I32), in_=src[0, f : 16 : 4, :].bitcast(I32))
             return plane
@@ -57,16 +59,16 @@ def tile_attend_gkeystore_kernel(tc, query, keys_words, keys_scales, gout, vals_
         def quantize(name, grouped, width):
             codes = sb.tile([P, width], U32, name=name + "_codes", align_bytes=64)
             scales = sb.tile([P, width], U8, name=name + "_scales", align_bytes=64)
-            nc.vector.quantize_mx(out=codes[:].bitcast(FP8X4), scales=scales[:], in_=grouped[:])
+            nc.vector.quantize_mx(out=codes[:].bitcast(FP8X4), scales=scales[:], in_=grouped)
             return codes, scales
 
         def deal(name, raw):
             grouped = sb.tile([P, PACK * Q], BF16, name=name + "_bf16", align_bytes=64)
-            nc.vector.tensor_copy(
-                out=grouped[:].rearrange("p (t s j) -> p s j t", t=PACK, j=PACK),
-                in_=raw[:].rearrange("p j (s t) -> p s j t", t=PACK),
-            )
-            return quantize(name, grouped, Q)
+            dst = grouped[:].rearrange("p (t s j) -> p s j t", t=PACK, j=PACK)
+            src = raw[:].rearrange("p j (s t) -> p s j t", t=PACK)
+            nc.vector.tensor_copy(out=dst[:, :DEAL_SPLIT], in_=src[:, :DEAL_SPLIT])
+            nc.scalar.copy(out=dst[:, DEAL_SPLIT:], in_=src[:, DEAL_SPLIT:])
+            return quantize(name, grouped[:], Q)
 
         def gather(name, words, plane):
             codes = sb.tile([P, I], U32, name=name + "_codes", align_bytes=64)
@@ -86,25 +88,29 @@ def tile_attend_gkeystore_kernel(tc, query, keys_words, keys_scales, gout, vals_
                 outs.append(o)
             return outs
 
+        def mx(o, lhs, rhs):
+            nc.tensor.matmul_mx(out=o, lhsT=lhs[0].bitcast(FP8X4), lhsT_scale=lhs[1],
+                                rhs=rhs[0].bitcast(FP8X4), rhs_scale=rhs[1], start=True, stop=True)
+
         def blocks(pair, n):
             return [(pair[0][:, b * P : (b + 1) * P], pair[1][:, b * P : (b + 1) * P]) for b in range(n)]
 
-        gout_raw = load_rows("gout_raw", gout, Q)
-        vals_plane = load_scales("vals_plane", vals_scales, VALS_PLANE)
+        vals_pool = load_words("vals_pool", vals_words)
+        fade_rows = sb.tile([P, P], F32, name="fade_rows")
+        nc.sync.dma_start(out=fade_rows[:], in_=fade.rearrange("o (b u) -> o b u", u=P).to_broadcast([P // UB, UB, P]))
         slots = lists.tile([P, I // 16], U16, name="slots")
         nc.sync.dma_start(slots[:], offs)
-        vals_pool = load_words("vals_pool", vals_words)
-        lse_c = load_column("lse_c", lse)
         delta_c = load_column("delta_c", delta)
         qs_c = load_column("qs_c", qs)
+        gout_raw = load_rows("gout_raw", gout, Q)
+        vals_plane = load_scales("vals_plane", vals_scales, VALS_PLANE, nc.gpsimd)
         query_raw = load_rows("query_raw", query, Q)
-        keys_plane = load_scales("keys_plane", keys_scales, 0)
+        keys_plane = load_scales("keys_plane", keys_scales, 0, nc.vector)
         keys_pool = load_words("keys_pool", keys_words)
+        lse_c = load_column("lse_c", lse)
         qrows_raw = [load_rows("qrows_raw" + str(h), qrows[:, h * HALF : (h + 1) * HALF], HALF) for h in range(2)]
         places = lists.tile([P, I // 16], U16, name="places")
         nc.sync.dma_start(places[:], offs2)
-        fade_rows = sb.tile([P, P], F32, name="fade_rows")
-        nc.sync.dma_start(out=fade_rows[:], in_=fade.rearrange("o (b u) -> o b u", u=P).to_broadcast([P // UB, UB, P]))
         old_t = []
         for j in range(PACK):
             o = sb.tile([P, U], F32, name="old" + str(j))
@@ -112,18 +118,27 @@ def tile_attend_gkeystore_kernel(tc, query, keys_words, keys_scales, gout, vals_
             old_t.append(o)
 
         windows = []
-        for j in range(2):
+        for j in range(3):
             w = sb.tile([P, U], F32, name="window" + str(j))
             nc.vector.memset(w[:], 0.0)
             windows.append(w)
+        windows.append(windows[1])
         ident = sb.tile([P, P], F32, name="ident")
         make_identity(nc, ident[:])
         neg_lse = sb.tile([P, PACK], F32, name="neg_lse")
-        nc.scalar.activation(out=neg_lse[:], in_=lse_c[:], func=ACT.Copy, scale=-1.0)
+        nc.gpsimd.tensor_scalar(out=neg_lse[:], in0=lse_c[:], scalar1=-1.0, scalar2=0.0, op0=ALU.mult, op1=ALU.add)
         fade_ps = ps.tile([P, PACK, P], F32, name="fade_ps", tag="turn0")
         nc.tensor.transpose(fade_ps[:, 0, :], fade_rows[:], ident[:])
         fade_c = sb.tile([P, UB], F32, name="fade_c")
         nc.vector.tensor_copy(out=fade_c[:], in_=fade_ps[:, 0, 0:UB])
+
+        fade_all = sb.tile([P, U], F32, name="fade_all")
+        for h in range(2):
+            spread = ps.tile([P, PACK, P], F32, name="spread", tag="back" + str(h))
+            for b in range(PACK):
+                ub = h * PACK + b
+                nc.tensor.transpose(spread[:, b, :], fade_c[:, ub : ub + 1].to_broadcast([P, P]), ident[:])
+            nc.scalar.copy(out=fade_all[:, h * BANK : (h + 1) * BANK], in_=spread[:].rearrange("p b u -> p (b u)"))
 
         gout_q = deal("gout", gout_raw)
         vals_g = gather("vals", vals_pool, vals_plane)
@@ -135,62 +150,94 @@ def tile_attend_gkeystore_kernel(tc, query, keys_words, keys_scales, gout, vals_
 
         query_q = deal("query", query_raw)
         keys_g = gather("keys", keys_pool, keys_plane)
-        a = scores("a", blocks(query_q, PACK), keys_g, 0)
-        weight = sb.tile([P, PACK, I], F32, name="weight")
-        for t in range(PACK):
-            nc.scalar.activation(out=weight[:, t, :], in_=a[t], func=ACT.Exp, bias=neg_lse[:, t : t + 1], scale=1.0)
+        query_b = blocks(query_q, PACK)
+        weights = []
+        for h in range(2):
+            a = ps.tile([P, PACK, SLOTS], F32, name="a" + str(h), tag="mx" + str(h))
+            cols = slice(h * SLOTS, (h + 1) * SLOTS)
+            for t in range(PACK):
+                mx(a[:, t, :], query_b[t], (keys_g[0][:, cols], keys_g[1][:, cols]))
+            weight = sb.tile([P, PACK, SLOTS], F32, name="weight" + str(h))
+            for t in range(PACK):
+                nc.scalar.activation(out=weight[:, t, :], in_=a[:, t, :], func=ACT.Exp, bias=neg_lse[:, t : t + 1], scale=1.0)
+            weights.append(weight)
 
-        def weave(h, engine_copy):
-            grouped = sb.tile([P, PACK * HALF], BF16, name="qrows_bf16_" + str(h), align_bytes=64)
-            engine_copy(
-                out=grouped[:].rearrange("p (c i j) -> p c j i", i=4, j=PACK),
-                in_=qrows_raw[h][:].rearrange("p j (c i) -> p c j i", i=4),
-            )
+        stage = sb.tile([P, PACK * (I + D)], BF16, name="stage", tag="stage", align_bytes=64)
+
+        def weave(h, engine_copy, pieces):
+            grouped = stage[:, PACK * (I + h * HALF) : PACK * (I + (h + 1) * HALF)]
+            width = HALF // pieces
+            for k in range(pieces):
+                engine_copy(
+                    out=grouped[:, PACK * k * width : PACK * (k + 1) * width].rearrange("p (c i j) -> p c j i", i=4, j=PACK),
+                    in_=qrows_raw[h][:, :, k * width : (k + 1) * width].rearrange("p j (c i) -> p c j i", i=4),
+                )
             return grouped
 
-        qrows_q = [quantize("qrows0", weave(0, nc.vector.tensor_copy), HALF)]
+        qrows_b = blocks(quantize("qrows0", weave(0, nc.vector.tensor_copy, 1), HALF), 2)
 
-        ds = sb.tile([P, PACK * I], BF16, name="ds", align_bytes=64)
-        nc.vector.tensor_tensor(
-            out=ds[:].rearrange("p (c i t) -> p c t i", i=4, t=PACK),
-            in0=weight[:].rearrange("p t (c i) -> p c t i", i=4),
-            in1=grad[:].rearrange("p t (c i) -> p c t i", i=4),
-            op=ALU.mult,
-        )
-        ds_q = quantize("ds", ds, I)
-        qrows_q.append(quantize("qrows1", weave(1, nc.scalar.copy), HALF))
-        dk = scores("dk", blocks(qrows_q[0], 2) + blocks(qrows_q[1], 2), ds_q, 0)
+        ds_codes = sb.tile([P, I], U32, name="ds_codes", align_bytes=64)
+        ds_scales = sb.tile([P, I], U8, name="ds_scales", align_bytes=64)
+        halves = [slice(h * SLOTS, (h + 1) * SLOTS) for h in range(2)]
+        ds = [stage[:, PACK * h * SLOTS : PACK * (h + 1) * SLOTS] for h in range(2)]
+        for h in range(2):
+            nc.vector.tensor_tensor(
+                out=ds[h].rearrange("p (c i t) -> p c t i", i=4, t=PACK),
+                in0=weights[h][:].rearrange("p t (c i) -> p c t i", i=4),
+                in1=grad[:, :, halves[h]].rearrange("p t (c i) -> p c t i", i=4),
+                op=ALU.mult,
+            )
+        for h in range(2):
+            nc.vector.quantize_mx(out=ds_codes[:, halves[h]].bitcast(FP8X4), scales=ds_scales[:, halves[h]], in_=ds[h])
 
-        dk_sb = []
-        for j in range(PACK):
-            d = sb.tile([P, I], F32, name="dk_sb" + str(j))
-            nc.scalar.copy(out=d[:], in_=dk[j])
-            dk_sb.append(d)
+        def scatter(j, cols, tag):
+            n = cols.stop - cols.start
+            dk = ps.tile([P, n], F32, name="dk", tag=tag)
+            mx(dk[:], qrows_b[j], (ds_codes[:, cols], ds_scales[:, cols]))
+            dk_sb = sb.tile([P, n], F32, name="dk_sb" + str(j) + "_" + str(cols.start))
+            nc.scalar.copy(out=dk_sb[:], in_=dk[:])
+            nc.vector.tensor_copy(out=windows[j][:].indirect(places[:, cols.start // 16 : cols.stop // 16]), in_=dk_sb[:])
 
-        def scatter(j):
-            nc.vector.tensor_copy(out=windows[j % 2][:].indirect(places[:]), in_=dk_sb[j][:])
+        def store(j, h, res):
+            nc.sync.dma_start(out=out[j * P : (j + 1) * P, h * BANK : (h + 1) * BANK], in_=res[:])
 
-        def finish(j):
-            faded_t = sb.tile([P, UB, P], F32, name="faded_t" + str(j))
-            for h in range(2):
-                turn = ps.tile([P, PACK, P], F32, name="turn", tag="turn" + str(h))
-                for b in range(PACK):
-                    ub = h * PACK + b
-                    nc.tensor.transpose(turn[:, b, :], old_t[j][:, ub * P : (ub + 1) * P], ident[:])
-                for b in range(PACK):
-                    ub = h * PACK + b
-                    nc.scalar.activation(out=faded_t[:, ub, :], in_=turn[:, b, :], func=ACT.Copy, scale=fade_c[:, ub : ub + 1])
-            for h in range(2):
-                back = ps.tile([P, BANK], F32, name="back", tag="back" + str(2 * (j % 2) + h))
-                for b in range(PACK):
-                    nc.tensor.transpose(back[:, b * P : (b + 1) * P], faded_t[:, h * PACK + b, :], ident[:])
+        def finish_gpsimd(j, nhalves):
+            faded = sb.tile([P, nhalves * BANK], F32, name="faded" + str(j), tag="stage", align_bytes=64)
+            nc.gpsimd.tensor_tensor(out=faded[:], in0=old_t[j][:, : nhalves * BANK], in1=fade_all[:, : nhalves * BANK], op=ALU.mult)
+            for h in range(nhalves):
                 cols = slice(h * BANK, (h + 1) * BANK)
                 res = sb.tile([P, BANK], F32, name="res" + str(2 * j + h))
-                nc.vector.tensor_tensor(out=res[:], in0=back[:], in1=windows[j % 2][:, cols], op=ALU.add)
-                nc.sync.dma_start(out=out[j * P : (j + 1) * P, cols], in_=res[:])
+                nc.gpsimd.tensor_tensor(out=res[:], in0=faded[:, cols], in1=windows[j][:, cols], op=ALU.add)
+                store(j, h, res)
 
-        scatter(0)
-        for j in range(PACK):
-            if j + 1 < PACK:
-                scatter(j + 1)
-            finish(j)
+        def finish_turned(j, h, turn_bank, bank):
+            faded_t = sb.tile([P, PACK, P], F32, name="faded_t" + str(2 * j + h))
+            turn = ps.tile([P, PACK, P], F32, name="turn", tag=turn_bank)
+            for b in range(PACK):
+                ub = h * PACK + b
+                nc.tensor.transpose(turn[:, b, :], old_t[j][:, ub * P : (ub + 1) * P], ident[:])
+            for b in range(PACK):
+                ub = h * PACK + b
+                nc.scalar.activation(out=faded_t[:, b, :], in_=turn[:, b, :], func=ACT.Copy, scale=fade_c[:, ub : ub + 1])
+            back = ps.tile([P, BANK], F32, name="back", tag=bank)
+            for b in range(PACK):
+                nc.tensor.transpose(back[:, b * P : (b + 1) * P], faded_t[:, b, :], ident[:])
+            cols = slice(h * BANK, (h + 1) * BANK)
+            res = sb.tile([P, BANK], F32, name="res" + str(2 * j + h))
+            nc.vector.tensor_tensor(out=res[:], in0=back[:], in1=windows[j][:, cols], op=ALU.add)
+            store(j, h, res)
+
+        every = slice(0, I)
+        scatter(0, halves[0], "mx0")
+        scatter(0, halves[1], "mx1")
+        scatter(1, every, "dk0")
+        qrows_b.extend(blocks(quantize("qrows1", weave(1, nc.scalar.copy, 2), HALF), 2))
+        scatter(2, every, "dk1")
+        finish_gpsimd(0, 2)
+        finish_turned(1, 0, "mx0", "back0")
+        finish_turned(1, 1, "mx1", "back1")
+        scatter(3, every, "dk2")
+        finish_gpsimd(2, 1)
+        finish_turned(2, 1, "mx0", "turn0")
+        finish_turned(3, 0, "mx1", "dk0")
+        finish_turned(3, 1, "mx0", "dk1")

@@ -23,7 +23,7 @@ UB = U // P
 VALS_PLANE = 4
 HALF = D // 2
 SLOTS = I // 2
-DEAL_SPLIT = 80
+SHARE = 768
 
 
 def tile_attend_gkeystore_kernel(tc, query, keys_words, keys_scales, gout, vals_words, vals_scales,
@@ -44,9 +44,9 @@ def tile_attend_gkeystore_kernel(tc, query, keys_words, keys_scales, gout, vals_
             nc.sync.dma_start(out=words[:].bitcast(I32), in_=src[0].rearrange("p n t -> p (n t)").bitcast(I32))
             return words
 
-        def load_scales(name, src, first, clear):
+        def load_scales(name, src, first):
             plane = sb.tile([P, T], U8, name=name)
-            clear.memset(plane[:].bitcast(I32), 0)
+            nc.vector.memset(plane[:].bitcast(I32), 0)
             for f in range(4):
                 nc.sync.dma_start(out=plane[first + f : P : 32, :].bitcast(I32), in_=src[0, f : 16 : 4, :].bitcast(I32))
             return plane
@@ -66,8 +66,7 @@ def tile_attend_gkeystore_kernel(tc, query, keys_words, keys_scales, gout, vals_
             grouped = sb.tile([P, PACK * Q], BF16, name=name + "_bf16", align_bytes=64)
             dst = grouped[:].rearrange("p (t s j) -> p s j t", t=PACK, j=PACK)
             src = raw[:].rearrange("p j (s t) -> p s j t", t=PACK)
-            nc.vector.tensor_copy(out=dst[:, :DEAL_SPLIT], in_=src[:, :DEAL_SPLIT])
-            nc.scalar.copy(out=dst[:, DEAL_SPLIT:], in_=src[:, DEAL_SPLIT:])
+            nc.vector.tensor_copy(out=dst, in_=src)
             return quantize(name, grouped[:], Q)
 
         def gather(name, words, plane):
@@ -95,19 +94,19 @@ def tile_attend_gkeystore_kernel(tc, query, keys_words, keys_scales, gout, vals_
         def blocks(pair, n):
             return [(pair[0][:, b * P : (b + 1) * P], pair[1][:, b * P : (b + 1) * P]) for b in range(n)]
 
-        vals_pool = load_words("vals_pool", vals_words)
+        gout_raw = load_rows("gout_raw", gout, Q)
         fade_rows = sb.tile([P, P], F32, name="fade_rows")
         nc.sync.dma_start(out=fade_rows[:], in_=fade.rearrange("o (b u) -> o b u", u=P).to_broadcast([P // UB, UB, P]))
+        vals_plane = load_scales("vals_plane", vals_scales, VALS_PLANE)
         slots = lists.tile([P, I // 16], U16, name="slots")
         nc.sync.dma_start(slots[:], offs)
+        vals_pool = load_words("vals_pool", vals_words)
         delta_c = load_column("delta_c", delta)
         qs_c = load_column("qs_c", qs)
-        gout_raw = load_rows("gout_raw", gout, Q)
-        vals_plane = load_scales("vals_plane", vals_scales, VALS_PLANE, nc.gpsimd)
         query_raw = load_rows("query_raw", query, Q)
-        keys_plane = load_scales("keys_plane", keys_scales, 0, nc.vector)
-        keys_pool = load_words("keys_pool", keys_words)
+        keys_plane = load_scales("keys_plane", keys_scales, 0)
         lse_c = load_column("lse_c", lse)
+        keys_pool = load_words("keys_pool", keys_words)
         qrows_raw = [load_rows("qrows_raw" + str(h), qrows[:, h * HALF : (h + 1) * HALF], HALF) for h in range(2)]
         places = lists.tile([P, I // 16], U16, name="places")
         nc.sync.dma_start(places[:], offs2)
@@ -127,6 +126,8 @@ def tile_attend_gkeystore_kernel(tc, query, keys_words, keys_scales, gout, vals_
         make_identity(nc, ident[:])
         neg_lse = sb.tile([P, PACK], F32, name="neg_lse")
         nc.gpsimd.tensor_scalar(out=neg_lse[:], in0=lse_c[:], scalar1=-1.0, scalar2=0.0, op0=ALU.mult, op1=ALU.add)
+        shift = sb.tile([P, PACK], F32, name="shift")
+        nc.vector.scalar_tensor_tensor(out=shift[:], in0=delta_c[:], scalar=-1.0, in1=qs_c[:], op0=ALU.mult, op1=ALU.mult)
         fade_ps = ps.tile([P, PACK, P], F32, name="fade_ps", tag="turn0")
         nc.tensor.transpose(fade_ps[:, 0, :], fade_rows[:], ident[:])
         fade_c = sb.tile([P, UB], F32, name="fade_c")
@@ -143,12 +144,11 @@ def tile_attend_gkeystore_kernel(tc, query, keys_words, keys_scales, gout, vals_
         gout_q = deal("gout", gout_raw)
         vals_g = gather("vals", vals_pool, vals_plane)
         dp = scores("dp", blocks(gout_q, PACK), vals_g, VALS_PLANE)
+        query_q = deal("query", query_raw)
         grad = sb.tile([P, PACK, I], F32, name="grad")
         for t in range(PACK):
-            nc.vector.tensor_scalar(out=grad[:, t, :], in0=dp[t], scalar1=delta_c[:, t : t + 1], scalar2=qs_c[:, t : t + 1],
-                                    op0=ALU.subtract, op1=ALU.mult)
+            nc.scalar.activation(out=grad[:, t, :], in_=dp[t], func=ACT.Identity, scale=qs_c[:, t : t + 1], bias=shift[:, t : t + 1])
 
-        query_q = deal("query", query_raw)
         keys_g = gather("keys", keys_pool, keys_plane)
         query_b = blocks(query_q, PACK)
         weights = []
@@ -164,31 +164,31 @@ def tile_attend_gkeystore_kernel(tc, query, keys_words, keys_scales, gout, vals_
 
         stage = sb.tile([P, PACK * (I + D)], BF16, name="stage", tag="stage", align_bytes=64)
 
-        def weave(h, engine_copy, pieces):
+        def weave(h):
             grouped = stage[:, PACK * (I + h * HALF) : PACK * (I + (h + 1) * HALF)]
-            width = HALF // pieces
-            for k in range(pieces):
-                engine_copy(
-                    out=grouped[:, PACK * k * width : PACK * (k + 1) * width].rearrange("p (c i j) -> p c j i", i=4, j=PACK),
-                    in_=qrows_raw[h][:, :, k * width : (k + 1) * width].rearrange("p j (c i) -> p c j i", i=4),
-                )
+            nc.vector.tensor_copy(
+                out=grouped.rearrange("p (c i j) -> p c j i", i=4, j=PACK),
+                in_=qrows_raw[h][:].rearrange("p j (c i) -> p c j i", i=4),
+            )
             return grouped
 
-        qrows_b = blocks(quantize("qrows0", weave(0, nc.vector.tensor_copy, 1), HALF), 2)
+        qrows_b = blocks(quantize("qrows0", weave(0), HALF), 2)
+        woven = weave(1)
 
         ds_codes = sb.tile([P, I], U32, name="ds_codes", align_bytes=64)
         ds_scales = sb.tile([P, I], U8, name="ds_scales", align_bytes=64)
         halves = [slice(h * SLOTS, (h + 1) * SLOTS) for h in range(2)]
-        ds = [stage[:, PACK * h * SLOTS : PACK * (h + 1) * SLOTS] for h in range(2)]
         for h in range(2):
+            ds = stage[:, PACK * h * SLOTS : PACK * (h + 1) * SLOTS]
             nc.vector.tensor_tensor(
-                out=ds[h].rearrange("p (c i t) -> p c t i", i=4, t=PACK),
+                out=ds.rearrange("p (c i t) -> p c t i", i=4, t=PACK),
                 in0=weights[h][:].rearrange("p t (c i) -> p c t i", i=4),
                 in1=grad[:, :, halves[h]].rearrange("p t (c i) -> p c t i", i=4),
                 op=ALU.mult,
             )
-        for h in range(2):
-            nc.vector.quantize_mx(out=ds_codes[:, halves[h]].bitcast(FP8X4), scales=ds_scales[:, halves[h]], in_=ds[h])
+            nc.vector.quantize_mx(out=ds_codes[:, halves[h]].bitcast(FP8X4), scales=ds_scales[:, halves[h]], in_=ds)
+            if h == 0:
+                qrows_b = qrows_b + blocks(quantize("qrows1", woven, HALF), 2)
 
         def scatter(j, cols, tag):
             n = cols.stop - cols.start
@@ -198,46 +198,44 @@ def tile_attend_gkeystore_kernel(tc, query, keys_words, keys_scales, gout, vals_
             nc.scalar.copy(out=dk_sb[:], in_=dk[:])
             nc.vector.tensor_copy(out=windows[j][:].indirect(places[:, cols.start // 16 : cols.stop // 16]), in_=dk_sb[:])
 
-        def store(j, h, res):
-            nc.sync.dma_start(out=out[j * P : (j + 1) * P, h * BANK : (h + 1) * BANK], in_=res[:])
+        def store(queue, j, cols, res):
+            queue.dma_start(out=out[j * P : (j + 1) * P, cols], in_=res[:])
 
-        def finish_gpsimd(j, nhalves):
-            faded = sb.tile([P, nhalves * BANK], F32, name="faded" + str(j), tag="stage", align_bytes=64)
-            nc.gpsimd.tensor_tensor(out=faded[:], in0=old_t[j][:, : nhalves * BANK], in1=fade_all[:, : nhalves * BANK], op=ALU.mult)
-            for h in range(nhalves):
-                cols = slice(h * BANK, (h + 1) * BANK)
-                res = sb.tile([P, BANK], F32, name="res" + str(2 * j + h))
+        def finish_gpsimd(j, width):
+            faded = sb.tile([P, width], F32, name="faded" + str(j), tag="stage", align_bytes=64)
+            nc.gpsimd.tensor_tensor(out=faded[:], in0=old_t[j][:, :width], in1=fade_all[:, :width], op=ALU.mult)
+            for lo in range(0, width, BANK):
+                cols = slice(lo, min(lo + BANK, width))
+                res = sb.tile([P, cols.stop - lo], F32, name="res" + str(j) + "_" + str(lo))
                 nc.gpsimd.tensor_tensor(out=res[:], in0=faded[:, cols], in1=windows[j][:, cols], op=ALU.add)
-                store(j, h, res)
+                store(nc.scalar, j, cols, res)
 
-        def finish_turned(j, h, turn_bank, bank):
-            faded_t = sb.tile([P, PACK, P], F32, name="faded_t" + str(2 * j + h))
-            turn = ps.tile([P, PACK, P], F32, name="turn", tag=turn_bank)
-            for b in range(PACK):
-                ub = h * PACK + b
-                nc.tensor.transpose(turn[:, b, :], old_t[j][:, ub * P : (ub + 1) * P], ident[:])
-            for b in range(PACK):
-                ub = h * PACK + b
+        def finish_turned(j, lo, hi, turn_bank, back_bank):
+            n = (hi - lo) // P
+            faded_t = sb.tile([P, n, P], F32, name="faded_t" + str(j) + "_" + str(lo))
+            turn = ps.tile([P, n, P], F32, name="turn", tag=turn_bank)
+            for b in range(n):
+                nc.tensor.transpose(turn[:, b, :], old_t[j][:, lo + b * P : lo + (b + 1) * P], ident[:])
+            for b in range(n):
+                ub = lo // P + b
                 nc.scalar.activation(out=faded_t[:, b, :], in_=turn[:, b, :], func=ACT.Copy, scale=fade_c[:, ub : ub + 1])
-            back = ps.tile([P, BANK], F32, name="back", tag=bank)
-            for b in range(PACK):
+            back = ps.tile([P, hi - lo], F32, name="back", tag=back_bank)
+            for b in range(n):
                 nc.tensor.transpose(back[:, b * P : (b + 1) * P], faded_t[:, b, :], ident[:])
-            cols = slice(h * BANK, (h + 1) * BANK)
-            res = sb.tile([P, BANK], F32, name="res" + str(2 * j + h))
-            nc.vector.tensor_tensor(out=res[:], in0=back[:], in1=windows[j][:, cols], op=ALU.add)
-            store(j, h, res)
+            res = sb.tile([P, hi - lo], F32, name="res" + str(j) + "_" + str(lo))
+            nc.vector.tensor_tensor(out=res[:], in0=back[:], in1=windows[j][:, lo:hi], op=ALU.add)
+            store(nc.sync, j, slice(lo, hi), res)
 
         every = slice(0, I)
         scatter(0, halves[0], "mx0")
         scatter(0, halves[1], "mx1")
         scatter(1, every, "dk0")
-        qrows_b.extend(blocks(quantize("qrows1", weave(1, nc.scalar.copy, 2), HALF), 2))
         scatter(2, every, "dk1")
-        finish_gpsimd(0, 2)
-        finish_turned(1, 0, "mx0", "back0")
-        finish_turned(1, 1, "mx1", "back1")
+        finish_gpsimd(0, U)
+        finish_turned(1, 0, BANK, "mx0", "back0")
+        finish_turned(1, BANK, U, "mx1", "back1")
         scatter(3, every, "dk2")
-        finish_gpsimd(2, 1)
-        finish_turned(2, 1, "mx0", "turn0")
-        finish_turned(3, 0, "mx1", "dk0")
-        finish_turned(3, 1, "mx0", "dk1")
+        finish_gpsimd(2, SHARE)
+        finish_turned(2, SHARE, U, "mx0", "turn0")
+        finish_turned(3, 0, BANK, "mx1", "dk0")
+        finish_turned(3, BANK, U, "mx0", "dk1")

@@ -198,8 +198,8 @@ def tile_attend_gkeystore_kernel(tc, query, keys_words, keys_scales, gout, vals_
             nc.scalar.copy(out=dk_sb[:], in_=dk[:])
             nc.vector.tensor_copy(out=windows[j][:].indirect(places[:, cols.start // 16 : cols.stop // 16]), in_=dk_sb[:])
 
-        def store(queue, j, cols, res):
-            queue.dma_start(out=out[j * P : (j + 1) * P, cols], in_=res[:])
+        def store(j, cols, res):
+            nc.sync.dma_start(out=out[j * P : (j + 1) * P, cols], in_=res[:])
 
         def finish_gpsimd(j, width):
             faded = sb.tile([P, width], F32, name="faded" + str(j), tag="stage", align_bytes=64)
@@ -208,7 +208,7 @@ def tile_attend_gkeystore_kernel(tc, query, keys_words, keys_scales, gout, vals_
                 cols = slice(lo, min(lo + BANK, width))
                 res = sb.tile([P, cols.stop - lo], F32, name="res" + str(j) + "_" + str(lo))
                 nc.gpsimd.tensor_tensor(out=res[:], in0=faded[:, cols], in1=windows[j][:, cols], op=ALU.add)
-                store(nc.scalar, j, cols, res)
+                store(j, cols, res)
 
         def finish_turned(j, lo, hi, turn_bank, back_bank):
             n = (hi - lo) // P
@@ -224,7 +224,7 @@ def tile_attend_gkeystore_kernel(tc, query, keys_words, keys_scales, gout, vals_
                 nc.tensor.transpose(back[:, b * P : (b + 1) * P], faded_t[:, b, :], ident[:])
             res = sb.tile([P, hi - lo], F32, name="res" + str(j) + "_" + str(lo))
             nc.vector.tensor_tensor(out=res[:], in0=back[:], in1=windows[j][:, lo:hi], op=ALU.add)
-            store(nc.sync, j, slice(lo, hi), res)
+            store(j, slice(lo, hi), res)
 
         every = slice(0, I)
         scatter(0, halves[0], "mx0")

from contextlib import ExitStack

import concourse.mybir as mybir
from concourse.masks import make_identity

D, E, T, I, U, Q = 512, 512, 2048, 256, 1024, 512
FLOPS = 2 * Q * I * D + 2 * Q * I * E + 2 * D * I * Q

F32 = mybir.dt.float32
BF16 = mybir.dt.bfloat16
I32 = mybir.dt.int32
U32 = mybir.dt.uint32
U16 = mybir.dt.uint16
U8 = mybir.dt.uint8
FP8X4 = mybir.dt.float8_e4m3fn_x4
ALU = mybir.AluOpType
ACT = mybir.ActivationFunctionType

P = 128
PACK = 4
BANK = 512
UB = U // P
VALS_PLANE = 4
HALF = D // 2
SLOTS = I // 2
SHARE = 768


def tile_attend_gkeystore_kernel(tc, query, keys_words, keys_scales, gout, vals_words, vals_scales,
                                  lse, delta, qs, qrows, old, fade, offs, offs2, out):
    nc = tc.nc
    with ExitStack() as ctx:
        lists = ctx.enter_context(tc.tile_pool(name="lists", bufs=1))
        sb = ctx.enter_context(tc.tile_pool(name="sb", bufs=1))
        ps = ctx.enter_context(tc.psum_pool(name="ps", bufs=1))

        def load_rows(name, src, width):
            raw = sb.tile([P, PACK, width], F32, name=name)
            nc.sync.dma_start(out=raw[:], in_=src.rearrange("(p j) w -> p j w", j=PACK))
            return raw

        def load_words(name, src):
            words = sb.tile([P, T], U32, name=name)
            nc.sync.dma_start(out=words[:].bitcast(I32), in_=src[0].rearrange("p n t -> p (n t)").bitcast(I32))
            return words

        def load_scales(name, src, first):
            plane = sb.tile([P, T], U8, name=name)
            nc.vector.memset(plane[:].bitcast(I32), 0)
            for f in range(4):
                nc.sync.dma_start(out=plane[first + f : P : 32, :].bitcast(I32), in_=src[0, f : 16 : 4, :].bitcast(I32))
            return plane

        def load_column(name, src):
            col = sb.tile([P, PACK], F32, name=name)
            nc.sync.dma_start(out=col[:], in_=src.rearrange("(p t) o -> p (t o)", t=PACK))
            return col

        def quantize(name, grouped, width):
            codes = sb.tile([P, width], U32, name=name + "_codes", align_bytes=64)
            scales = sb.tile([P, width], U8, name=name + "_scales", align_bytes=64)
            nc.vector.quantize_mx(out=codes[:].bitcast(FP8X4), scales=scales[:], in_=grouped)
            return codes, scales

        def deal(name, raw):
            grouped = sb.tile([P, PACK * Q], BF16, name=name + "_bf16", align_bytes=64)
            dst = grouped[:].rearrange("p (t s j) -> p s j t", t=PACK, j=PACK)
            src = raw[:].rearrange("p j (s t) -> p s j t", t=PACK)
            nc.vector.tensor_copy(out=dst, in_=src)
            return quantize(name, grouped[:], Q)

        def gather(name, words, plane):
            codes = sb.tile([P, I], U32, name=name + "_codes", align_bytes=64)
            scales = sb.tile([P, I], U8, name=name + "_scales", align_bytes=64)
            nc.vector.tensor_copy(out=scales[:], in_=plane[:].indirect(slots[:]))
            nc.vector.tensor_copy(out=codes[:], in_=words[:].indirect(slots[:]))
            return codes, scales

        def scores(name, lhs, rhs, first):
            banks = [ps.tile([P, 2, I], F32, name=name + str(h), tag="mx" + str(h)) for h in range(2)]
            outs = []
            for t in range(PACK):
                cols = slice(t * P, (t + 1) * P)
                o = banks[t // 2][:, t % 2, :]
                nc.tensor.matmul_mx(out=o, lhsT=lhs[t][0].bitcast(FP8X4), lhsT_scale=lhs[t][1],
                                    rhs=rhs[0][:].bitcast(FP8X4), rhs_scale=rhs[1][first:P, :], start=True, stop=True)
                outs.append(o)
            return outs

        def mx(o, lhs, rhs):
            nc.tensor.matmul_mx(out=o, lhsT=lhs[0].bitcast(FP8X4), lhsT_scale=lhs[1],
                                rhs=rhs[0].bitcast(FP8X4), rhs_scale=rhs[1], start=True, stop=True)

        def blocks(pair, n):
            return [(pair[0][:, b * P : (b + 1) * P], pair[1][:, b * P : (b + 1) * P]) for b in range(n)]

        gout_raw = load_rows("gout_raw", gout, Q)
        fade_rows = sb.tile([P, P], F32, name="fade_rows")
        nc.sync.dma_start(out=fade_rows[:], in_=fade.rearrange("o (b u) -> o b u", u=P).to_broadcast([P // UB, UB, P]))
        vals_plane = load_scales("vals_plane", vals_scales, VALS_PLANE)
        slots = lists.tile([P, I // 16], U16, name="slots")
        nc.sync.dma_start(slots[:], offs)
        vals_pool = load_words("vals_pool", vals_words)
        delta_c = load_column("delta_c", delta)
        qs_c = load_column("qs_c", qs)
        query_raw = load_rows("query_raw", query, Q)
        keys_plane = load_scales("keys_plane", keys_scales, 0)
        lse_c = load_column("lse_c", lse)
        keys_pool = load_words("keys_pool", keys_words)
        qrows_raw = [load_rows("qrows_raw" + str(h), qrows[:, h * HALF : (h + 1) * HALF], HALF) for h in range(2)]
        places = lists.tile([P, I // 16], U16, name="places")
        nc.sync.dma_start(places[:], offs2)
        old_t = []
        for j in range(PACK):
            o = sb.tile([P, U], F32, name="old" + str(j))
            nc.sync.dma_start(out=o[:], in_=old[j * P : (j + 1) * P, :])
            old_t.append(o)

        windows = []
        for j in range(3):
            w = sb.tile([P, U], F32, name="window" + str(j))
            nc.vector.memset(w[:], 0.0)
            windows.append(w)
        windows.append(windows[1])
        ident = sb.tile([P, P], F32, name="ident")
        make_identity(nc, ident[:])
        neg_lse = sb.tile([P, PACK], F32, name="neg_lse")
        nc.gpsimd.tensor_scalar(out=neg_lse[:], in0=lse_c[:], scalar1=-1.0, scalar2=0.0, op0=ALU.mult, op1=ALU.add)
        shift = sb.tile([P, PACK], F32, name="shift")
        nc.vector.scalar_tensor_tensor(out=shift[:], in0=delta_c[:], scalar=-1.0, in1=qs_c[:], op0=ALU.mult, op1=ALU.mult)
        fade_ps = ps.tile([P, PACK, P], F32, name="fade_ps", tag="turn0")
        nc.tensor.transpose(fade_ps[:, 0, :], fade_rows[:], ident[:])
        fade_c = sb.tile([P, UB], F32, name="fade_c")
        nc.vector.tensor_copy(out=fade_c[:], in_=fade_ps[:, 0, 0:UB])

        fade_all = sb.tile([P, U], F32, name="fade_all")
        for h in range(2):
            spread = ps.tile([P, PACK, P], F32, name="spread", tag="back" + str(h))
            for b in range(PACK):
                ub = h * PACK + b
                nc.tensor.transpose(spread[:, b, :], fade_c[:, ub : ub + 1].to_broadcast([P, P]), ident[:])
            nc.scalar.copy(out=fade_all[:, h * BANK : (h + 1) * BANK], in_=spread[:].rearrange("p b u -> p (b u)"))

        gout_q = deal("gout", gout_raw)
        vals_g = gather("vals", vals_pool, vals_plane)
        dp = scores("dp", blocks(gout_q, PACK), vals_g, VALS_PLANE)
        query_q = deal("query", query_raw)
        grad = sb.tile([P, PACK, I], F32, name="grad")
        for t in range(PACK):
            nc.scalar.activation(out=grad[:, t, :], in_=dp[t], func=ACT.Identity, scale=qs_c[:, t : t + 1], bias=shift[:, t : t + 1])

        keys_g = gather("keys", keys_pool, keys_plane)
        query_b = blocks(query_q, PACK)
        weights = []
        for h in range(2):
            a = ps.tile([P, PACK, SLOTS], F32, name="a" + str(h), tag="mx" + str(h))
            cols = slice(h * SLOTS, (h + 1) * SLOTS)
            for t in range(PACK):
                mx(a[:, t, :], query_b[t], (keys_g[0][:, cols], keys_g[1][:, cols]))
            weight = sb.tile([P, PACK, SLOTS], F32, name="weight" + str(h))
            for t in range(PACK):
                nc.scalar.activation(out=weight[:, t, :], in_=a[:, t, :], func=ACT.Exp, bias=neg_lse[:, t : t + 1], scale=1.0)
            weights.append(weight)

        stage = sb.tile([P, PACK * (I + D)], BF16, name="stage", tag="stage", align_bytes=64)

        def weave(h):
            grouped = stage[:, PACK * (I + h * HALF) : PACK * (I + (h + 1) * HALF)]
            nc.vector.tensor_copy(
                out=grouped.rearrange("p (c i j) -> p c j i", i=4, j=PACK),
                in_=qrows_raw[h][:].rearrange("p j (c i) -> p c j i", i=4),
            )
            return grouped

        qrows_b = blocks(quantize("qrows0", weave(0), HALF), 2)
        woven = weave(1)

        ds_codes = sb.tile([P, I], U32, name="ds_codes", align_bytes=64)
        ds_scales = sb.tile([P, I], U8, name="ds_scales", align_bytes=64)
        halves = [slice(h * SLOTS, (h + 1) * SLOTS) for h in range(2)]
        for h in range(2):
            ds = stage[:, PACK * h * SLOTS : PACK * (h + 1) * SLOTS]
            nc.vector.tensor_tensor(
                out=ds.rearrange("p (c i t) -> p c t i", i=4, t=PACK),
                in0=weights[h][:].rearrange("p t (c i) -> p c t i", i=4),
                in1=grad[:, :, halves[h]].rearrange("p t (c i) -> p c t i", i=4),
                op=ALU.mult,
            )
            nc.vector.quantize_mx(out=ds_codes[:, halves[h]].bitcast(FP8X4), scales=ds_scales[:, halves[h]], in_=ds)
            if h == 0:
                qrows_b = qrows_b + blocks(quantize("qrows1", woven, HALF), 2)

        def scatter(j, cols, tag):
            n = cols.stop - cols.start
            dk = ps.tile([P, n], F32, name="dk", tag=tag)
            mx(dk[:], qrows_b[j], (ds_codes[:, cols], ds_scales[:, cols]))
            dk_sb = sb.tile([P, n], F32, name="dk_sb" + str(j) + "_" + str(cols.start))
            nc.scalar.copy(out=dk_sb[:], in_=dk[:])
            nc.vector.tensor_copy(out=windows[j][:].indirect(places[:, cols.start // 16 : cols.stop // 16]), in_=dk_sb[:])

        def store(j, cols, res):
            nc.sync.dma_start(out=out[j * P : (j + 1) * P, cols], in_=res[:])

        def finish_gpsimd(j, width):
            faded = sb.tile([P, width], F32, name="faded" + str(j), tag="stage", align_bytes=64)
            nc.gpsimd.tensor_tensor(out=faded[:], in0=old_t[j][:, :width], in1=fade_all[:, :width], op=ALU.mult)
            for lo in range(0, width, BANK):
                cols = slice(lo, min(lo + BANK, width))
                res = sb.tile([P, cols.stop - lo], F32, name="res" + str(j) + "_" + str(lo))
                nc.gpsimd.tensor_tensor(out=res[:], in0=faded[:, cols], in1=windows[j][:, cols], op=ALU.add)
                store(j, cols, res)

        def finish_turned(j, lo, hi, turn_bank, back_bank):
            n = (hi - lo) // P
            faded_t = sb.tile([P, n, P], F32, name="faded_t" + str(j) + "_" + str(lo))
            turn = ps.tile([P, n, P], F32, name="turn", tag=turn_bank)
            for b in range(n):
                nc.tensor.transpose(turn[:, b, :], old_t[j][:, lo + b * P : lo + (b + 1) * P], ident[:])
            for b in range(n):
                ub = lo // P + b
                nc.scalar.activation(out=faded_t[:, b, :], in_=turn[:, b, :], func=ACT.Copy, scale=fade_c[:, ub : ub + 1])
            back = ps.tile([P, hi - lo], F32, name="back", tag=back_bank)
            for b in range(n):
                nc.tensor.transpose(back[:, b * P : (b + 1) * P], faded_t[:, b, :], ident[:])
            res = sb.tile([P, hi - lo], F32, name="res" + str(j) + "_" + str(lo))
            nc.vector.tensor_tensor(out=res[:], in0=back[:], in1=windows[j][:, lo:hi], op=ALU.add)
            store(j, slice(lo, hi), res)

        every = slice(0, I)
        scatter(0, halves[0], "mx0")
        scatter(0, halves[1], "mx1")
        scatter(1, every, "dk0")
        scatter(2, every, "dk1")
        finish_gpsimd(0, U)
        finish_turned(1, 0, BANK, "mx0", "back0")
        finish_turned(1, BANK, U, "mx1", "back1")
        scatter(3, every, "dk2")
        finish_gpsimd(2, SHARE)
        finish_turned(2, SHARE, U, "mx0", "turn0")
        finish_turned(3, 0, BANK, "mx1", "dk0")
        finish_turned(3, BANK, U, "mx0", "dk1")
